import numpy as np
CORES = [17,41,65,89]
N = 4
def setup_inputs(rng):
    return {"x": rng.standard_normal((N, 128, 4096), dtype=np.float32)}
def reference(x):
    b = 4096 // N
    blocks = x.reshape(N, 128, N, b)
    return {"y": np.ascontiguousarray(blocks.transpose(2, 1, 0, 3)).reshape(N, 128, 4096)}

@@ -1,0 +1,140 @@
+import concourse.bass as bass
+
+NB = 1024
+
+SCRATCH = {
+    "out": ("sbuf", [128, 4096], "float32"),
+    "land": ("sbuf", [128, 4096], "float32"),
+    "rel": ("sbuf", [128, 1024], "float32"),
+}
+SEMAPHORES = ["ld0", "ld1", "ld2", "ld3", "ld4", "ld5", "st", "sent",
+              "a0", "a1", "a2", "a3", "a4", "a5", "a6", "a7", "a8", "a9", "a10", "a11",
+              "a12", "a13", "a14", "a15", "a16", "a17", "a18", "a19", "a20", "a21", "a22", "a23"]
+
+
+def peer(role, s):
+    if role == "S":
+        return s ^ 2
+    if role == "A":
+        return s ^ 1
+    return 3 - s
+
+
+def design():
+    w = NB // 4
+    pieces = []
+
+    def add(role, q, wave, lane, relays):
+        pieces.append(dict(role=role, c0=q * w, c1=(q + 1) * w, wave=wave, mask0=0xF << (4 * lane), relays=relays))
+
+    for die in (0, 1):
+        sw = (4, 5, 4) if die == 0 else (0, 0, 0)
+        mt = (6, 7, 6) if die == 0 else (2, 3, 2)
+        add("B", 0 + die, 0, 0 + die, [("src", sw[0]), ("dstmate", mt[0])])
+        add("A", 0 + die, 0, 2 + die, [("src", mt[0])])
+        add("S", 2 + die, 1, 0 + die, [("src", mt[1]), ("dstmate", mt[1])])
+        add("S", 0 + die, 1, 2 + die, [("src", sw[1])])
+        add("B", 2 + die, 2, 0 + die, [("src", sw[2]), ("dstmate", mt[2])])
+        add("A", 2 + die, 2, 2 + die, [("src", mt[2])])
+    loads = [("B", 0, 512), ("A", 0, 512), ("S", 0, 1024), ("B", 512, 1024), ("A", 512, 1024)]
+    stores = [("A", 0, 512), ("B", 0, 512), ("S", 0, 512), ("S", 512, 1024), ("A", 512, 1024), ("B", 512, 1024)]
+    return pieces, loads, stores
+
+
+def bits(m):
+    return bin(m).count("1")
+
+
+def build(cores):
+    pieces, loads, stores = design()
+    slot, nsem, hops = {}, {}, []
+    for s in range(4):
+        for p in pieces:
+            d = peer(p["role"], s)
+            seq = [cores[s]]
+            for where, k in p["relays"]:
+                ch = cores[s] // 8 if where == "src" else (cores[d] // 8) ^ 1
+                seq.append(ch * 8 + k)
+            seq.append(cores[d])
+            src = ("out", d * NB + p["c0"], d * NB + p["c1"])
+            prev = None
+            for h in range(len(seq) - 1):
+                a, b = seq[h], seq[h + 1]
+                if h == len(seq) - 2:
+                    dst = ("land", s * NB + p["c0"], s * NB + p["c1"])
+                else:
+                    o = slot.get(b, 0)
+                    slot[b] = o + p["c1"] - p["c0"]
+                    dst = ("rel", o, slot[b])
+                if h == 0:
+                    mask = p["mask0"]
+                else:
+                    mask = 0xFFFF if a // 8 == b // 8 else 0x00FF
+                sem = nsem.get(b, 0)
+                nsem[b] = sem + 1
+                hop = dict(frm=a, to=b, src=src, dst=dst, mask=mask, sem=sem, prev=prev, first=(h == 0),
+                           last=(h == len(seq) - 2), wave=p["wave"], role=p["role"], c0=p["c0"], c1=p["c1"], s=s, d=d)
+                hops.append(hop)
+                prev = hop
+                src = dst
+    return hops, loads, stores
+
+
+def rank_program(g, core, T, topo):
+    cores = list(T.cores)
+    hops, loads, stores = build(cores)
+    mine = [h for h in hops if h["frm"] == core]
+    if not mine:
+        return
+    arr = [T.sem.a0, T.sem.a1, T.sem.a2, T.sem.a3, T.sem.a4, T.sem.a5, T.sem.a6, T.sem.a7,
+           T.sem.a8, T.sem.a9, T.sem.a10, T.sem.a11, T.sem.a12, T.sem.a13, T.sem.a14, T.sem.a15,
+           T.sem.a16, T.sem.a17, T.sem.a18, T.sem.a19, T.sem.a20, T.sem.a21, T.sem.a22, T.sem.a23]
+    buf = {"out": T.out, "land": T.land, "rel": T.rel}
+
+    def ap(spec):
+        return buf[spec[0]][:, spec[1]:spec[2]]
+
+    def send(group):
+        if len(group) == 1:
+            h = group[0]
+            rid, pid, se = topo.addr(h["to"])
+            g.remote_dma(ap(h["dst"]), ap(h["src"]), arr[h["sem"]], T.sem.sent, pid, rid, h["mask"])
+        else:
+            trs = []
+            for h in group:
+                rid, pid, se = topo.addr(h["to"])
+                trs.append(bass.RemoteDMATransfer(dst_ids=[bass.DstId(rid=rid, pnc=pid)], dma_engine_mask=h["mask"],
+                                                  remote_sem=arr[h["sem"]], src=ap(h["src"]), dst=ap(h["dst"])))
+            g.remote_dma_fused(trs, local_sem=T.sem.sent)
+        return sum(bits(h["mask"]) for h in group)
+
+    sent = 0
+    r = T.rank_of(core)
+    if r is None:
+        for h in sorted(mine, key=lambda h: h["wave"]):
+            g.wait_ge(arr[h["prev"]["sem"]], bits(h["prev"]["mask"]))
+            sent += send([h])
+        g.wait_ge(T.sem.sent, sent)
+        return
+
+    lds = [T.sem.ld0, T.sem.ld1, T.sem.ld2, T.sem.ld3, T.sem.ld4, T.sem.ld5]
+    waves = sorted(set(h["wave"] for h in mine))
+    nld = {}
+    for role, a, b in loads:
+        o = peer(role, r) * NB
+        wave = min(h["wave"] for h in mine if h["role"] == role and a <= h["c0"] and h["c1"] <= b)
+        nld[wave] = nld.get(wave, 0) + 1
+        g.dma_start(T.out[:, o + a:o + b], T.x[:, o + a:o + b]).then_inc(lds[wave], 16)
+    for wave in waves:
+        if wave in nld:
+            g.wait_ge(lds[wave], 16 * nld[wave])
+        sent += send([h for h in mine if h["wave"] == wave])
+    g.dma_start(T.y[:, r * NB:(r + 1) * NB], T.x[:, r * NB:(r + 1) * NB]).then_inc(T.sem.st, 16)
+    for role, a, b in stores:
+        s = peer(role, r)
+        for h in hops:
+            if h["last"] and h["to"] == core and h["s"] == s and a <= h["c0"] and h["c1"] <= b:
+                g.wait_ge(arr[h["sem"]], bits(h["mask"]))
+        g.dma_start(T.y[:, s * NB + a:s * NB + b], T.land[:, s * NB + a:s * NB + b]).then_inc(T.sem.st, 16)
+    g.wait_ge(T.sem.st, 16 * (len(stores) + 1))
+    g.wait_ge(T.sem.sent, sent)

@@ -1,13 +1,15 @@
 import concourse.bass as bass
 
 NB = 1024
+DESIGN = "blk"
+AHEAD = 9
 
 SCRATCH = {
     "out": ("sbuf", [128, 4096], "float32"),
     "land": ("sbuf", [128, 4096], "float32"),
-    "rel": ("sbuf", [128, 1024], "float32"),
+    "rel": ("sbuf", [128, 2048], "float32"),
 }
-SEMAPHORES = ["ld0", "ld1", "ld2", "ld3", "ld4", "ld5", "st", "sent",
+SEMAPHORES = ["ld0", "ld1", "ld2", "ld3", "ld4", "ld5", "ld6", "ld7", "st", "sent",
               "a0", "a1", "a2", "a3", "a4", "a5", "a6", "a7", "a8", "a9", "a10", "a11",
               "a12", "a13", "a14", "a15", "a16", "a17", "a18", "a19", "a20", "a21", "a22", "a23"]
 
@@ -21,23 +23,36 @@ def peer(role, s):
 
 
 def design():
-    w = NB // 4
     pieces = []
 
-    def add(role, q, wave, lane, relays):
-        pieces.append(dict(role=role, c0=q * w, c1=(q + 1) * w, wave=wave, mask0=0xF << (4 * lane), relays=relays))
+    def add(role, c0, c1, wave, mask0, relays):
+        pieces.append(dict(role=role, c0=c0, c1=c1, wave=wave, mask0=mask0, relays=relays))
 
-    for die in (0, 1):
-        sw = (4, 5, 4) if die == 0 else (0, 0, 0)
-        mt = (6, 7, 6) if die == 0 else (2, 3, 2)
-        add("B", 0 + die, 0, 0 + die, [("src", sw[0]), ("dstmate", mt[0])])
-        add("A", 0 + die, 0, 2 + die, [("src", mt[0])])
-        add("S", 2 + die, 1, 0 + die, [("src", mt[1]), ("dstmate", mt[1])])
-        add("S", 0 + die, 1, 2 + die, [("src", sw[1])])
-        add("B", 2 + die, 2, 0 + die, [("src", sw[2]), ("dstmate", mt[2])])
-        add("A", 2 + die, 2, 2 + die, [("src", mt[2])])
-    loads = [("B", 0, 512), ("A", 0, 512), ("S", 0, 1024), ("B", 512, 1024), ("A", 512, 1024)]
-    stores = [("A", 0, 512), ("B", 0, 512), ("S", 0, 512), ("S", 512, 1024), ("A", 512, 1024), ("B", 512, 1024)]
+    w = NB // 4
+    if DESIGN == "bal":
+        for die in (0, 1):
+            sw = (4, 5, 4) if die == 0 else (0, 0, 0)
+            mt = (6, 7, 6) if die == 0 else (2, 3, 2)
+            lo, hi = 0xF << (4 * die), 0xF << (4 * (2 + die))
+            add("B", (0 + die) * w, (1 + die) * w, 0, lo, [("src", sw[0]), ("dstmate", mt[0])])
+            add("A", (0 + die) * w, (1 + die) * w, 0, hi, [("src", mt[0])])
+            add("S", (2 + die) * w, (3 + die) * w, 1, lo, [("src", mt[1]), ("dstmate", mt[1])])
+            add("S", (0 + die) * w, (1 + die) * w, 1, hi, [("src", sw[1])])
+            add("B", (2 + die) * w, (3 + die) * w, 2, lo, [("src", sw[2]), ("dstmate", mt[2])])
+            add("A", (2 + die) * w, (3 + die) * w, 2, hi, [("src", mt[2])])
+        loads = [("B", 0, 512), ("A", 0, 512), ("S", 0, 1024), ("B", 512, 1024), ("A", 512, 1024)]
+        stores = [("A", 0, 512), ("B", 0, 512), ("S", 0, 512), ("S", 512, 1024), ("A", 512, 1024), ("B", 512, 1024)]
+    else:
+        for q, (h, m) in enumerate(((4, 6), (5, 7), (0, 2), (3, 3))):
+            add("B", q * w, (q + 1) * w, 0, 0xF << (4 * q), [("src", h), ("dstmate", m)])
+        add("S", 0 * w, 1 * w, 1, 0x000F, [("src", 4)])
+        add("S", 1 * w, 2 * w, 1, 0x00F0, [("src", 0)])
+        add("S", 2 * w, 3 * w, 1, 0x0F00, [("src", 7), ("dstmate", 6)])
+        add("S", 3 * w, 4 * w, 1, 0xF000, [("src", 2), ("dstmate", 2)])
+        for q, h in enumerate((6, 7, 2, 3)):
+            add("A", q * w, (q + 1) * w, 2, 0xF << (4 * q), [("src", h)])
+        loads = [("B", 0, 1024), ("S", 0, 1024), ("A", 0, 1024)]
+        stores = [("S", 0, 512), ("B", 0, 1024), ("A", 0, 1024), ("S", 512, 1024)]
     return pieces, loads, stores
 
 
@@ -117,15 +132,24 @@ def rank_program(g, core, T, topo):
         g.wait_ge(T.sem.sent, sent)
         return
 
-    lds = [T.sem.ld0, T.sem.ld1, T.sem.ld2, T.sem.ld3, T.sem.ld4, T.sem.ld5]
+    lds = [T.sem.ld0, T.sem.ld1, T.sem.ld2, T.sem.ld3, T.sem.ld4, T.sem.ld5, T.sem.ld6, T.sem.ld7]
     waves = sorted(set(h["wave"] for h in mine))
-    nld = {}
+    nld, ldw = {}, {}
     for role, a, b in loads:
-        o = peer(role, r) * NB
         wave = min(h["wave"] for h in mine if h["role"] == role and a <= h["c0"] and h["c1"] <= b)
         nld[wave] = nld.get(wave, 0) + 1
-        g.dma_start(T.out[:, o + a:o + b], T.x[:, o + a:o + b]).then_inc(lds[wave], 16)
-    for wave in waves:
+        ldw.setdefault(wave, []).append((role, a, b))
+
+    def load(wave):
+        for role, a, b in ldw.get(wave, []):
+            o = peer(role, r) * NB
+            g.dma_start(T.out[:, o + a:o + b], T.x[:, o + a:o + b]).then_inc(lds[wave], 16)
+
+    for wave in waves[:AHEAD]:
+        load(wave)
+    for i, wave in enumerate(waves):
+        if i + AHEAD < len(waves):
+            load(waves[i + AHEAD])
         if wave in nld:
             g.wait_ge(lds[wave], 16 * nld[wave])
         sent += send([h for h in mine if h["wave"] == wave])

@@ -1,7 +1,7 @@
 import concourse.bass as bass
 
 NB = 1024
-DESIGN = "blk"
+DESIGN = "opt1"
 AHEAD = 9
 
 SCRATCH = {
@@ -29,19 +29,16 @@ def design():
         pieces.append(dict(role=role, c0=c0, c1=c1, wave=wave, mask0=mask0, relays=relays))
 
     w = NB // 4
-    if DESIGN == "bal":
-        for die in (0, 1):
-            sw = (4, 5, 4) if die == 0 else (0, 0, 0)
-            mt = (6, 7, 6) if die == 0 else (2, 3, 2)
-            lo, hi = 0xF << (4 * die), 0xF << (4 * (2 + die))
-            add("B", (0 + die) * w, (1 + die) * w, 0, lo, [("src", sw[0]), ("dstmate", mt[0])])
-            add("A", (0 + die) * w, (1 + die) * w, 0, hi, [("src", mt[0])])
-            add("S", (2 + die) * w, (3 + die) * w, 1, lo, [("src", mt[1]), ("dstmate", mt[1])])
-            add("S", (0 + die) * w, (1 + die) * w, 1, hi, [("src", sw[1])])
-            add("B", (2 + die) * w, (3 + die) * w, 2, lo, [("src", sw[2]), ("dstmate", mt[2])])
-            add("A", (2 + die) * w, (3 + die) * w, 2, hi, [("src", mt[2])])
-        loads = [("B", 0, 512), ("A", 0, 512), ("S", 0, 1024), ("B", 512, 1024), ("A", 512, 1024)]
-        stores = [("A", 0, 512), ("B", 0, 512), ("S", 0, 512), ("S", 512, 1024), ("A", 512, 1024), ("B", 512, 1024)]
+    if DESIGN == "opt1":
+        for k in (0, 1):
+            add("B", (2 * k) * w, (2 * k + 1) * w, k, 0x000F, [("src", 4 + k), ("dstmate", 6 + k)])
+            add("B", (2 * k + 1) * w, (2 * k + 2) * w, k, 0x00F0, [("src", 0), ("dstmate", 2 + k)])
+            add("A", (2 * k) * w, (2 * k + 1) * w, k, 0x0F00, [("src", 6 + k)])
+            add("A", (2 * k + 1) * w, (2 * k + 2) * w, k, 0xF000, [("src", 2 + k)])
+            add("S", (2 * k) * w, (2 * k + 1) * w, 2, 0x000F << (8 * k), [("src", 4)])
+            add("S", (2 * k + 1) * w, (2 * k + 2) * w, 2, 0x00F0 << (8 * k), [("src", 2)])
+        loads = [("B", 0, 512), ("A", 0, 512), ("B", 512, 1024), ("A", 512, 1024), ("S", 0, 1024)]
+        stores = [("A", 0, 1024), ("B", 0, 512), ("S", 0, 512), ("B", 512, 1024), ("S", 512, 1024)]
     else:
         for q, (h, m) in enumerate(((4, 6), (5, 7), (0, 2), (3, 3))):
             add("B", q * w, (q + 1) * w, 0, 0xF << (4 * q), [("src", h), ("dstmate", m)])

@@ -1,17 +1,14 @@
 import concourse.bass as bass
 
 NB = 1024
-DESIGN = "opt1"
-AHEAD = 9
 
 SCRATCH = {
     "out": ("sbuf", [128, 4096], "float32"),
     "land": ("sbuf", [128, 4096], "float32"),
-    "rel": ("sbuf", [128, 2048], "float32"),
+    "rel": ("sbuf", [128, 1024], "float32"),
 }
-SEMAPHORES = ["ld0", "ld1", "ld2", "ld3", "ld4", "ld5", "ld6", "ld7", "st", "sent",
-              "a0", "a1", "a2", "a3", "a4", "a5", "a6", "a7", "a8", "a9", "a10", "a11",
-              "a12", "a13", "a14", "a15", "a16", "a17", "a18", "a19", "a20", "a21", "a22", "a23"]
+SEMAPHORES = ["ld0", "ld1", "ld2", "st", "sent",
+              "a0", "a1", "a2", "a3", "a4", "a5", "a6", "a7", "a8", "a9", "a10", "a11"]
 
 
 def peer(role, s):
@@ -25,31 +22,19 @@ def peer(role, s):
 def design():
     pieces = []
 
-    def add(role, c0, c1, wave, mask0, relays):
-        pieces.append(dict(role=role, c0=c0, c1=c1, wave=wave, mask0=mask0, relays=relays))
+    def add(role, q, wave, mask0, relays):
+        pieces.append(dict(role=role, c0=q * w, c1=(q + 1) * w, wave=wave, mask0=mask0, relays=relays))
 
     w = NB // 4
-    if DESIGN == "opt1":
-        for k in (0, 1):
-            add("B", (2 * k) * w, (2 * k + 1) * w, k, 0x000F, [("src", 4 + k), ("dstmate", 6 + k)])
-            add("B", (2 * k + 1) * w, (2 * k + 2) * w, k, 0x00F0, [("src", 0), ("dstmate", 2 + k)])
-            add("A", (2 * k) * w, (2 * k + 1) * w, k, 0x0F00, [("src", 6 + k)])
-            add("A", (2 * k + 1) * w, (2 * k + 2) * w, k, 0xF000, [("src", 2 + k)])
-            add("S", (2 * k) * w, (2 * k + 1) * w, 2, 0x000F << (8 * k), [("src", 4)])
-            add("S", (2 * k + 1) * w, (2 * k + 2) * w, 2, 0x00F0 << (8 * k), [("src", 2)])
-        loads = [("B", 0, 512), ("A", 0, 512), ("B", 512, 1024), ("A", 512, 1024), ("S", 0, 1024)]
-        stores = [("A", 0, 1024), ("B", 0, 512), ("S", 0, 512), ("B", 512, 1024), ("S", 512, 1024)]
-    else:
-        for q, (h, m) in enumerate(((4, 6), (5, 7), (0, 2), (3, 3))):
-            add("B", q * w, (q + 1) * w, 0, 0xF << (4 * q), [("src", h), ("dstmate", m)])
-        add("S", 0 * w, 1 * w, 1, 0x000F, [("src", 4)])
-        add("S", 1 * w, 2 * w, 1, 0x00F0, [("src", 0)])
-        add("S", 2 * w, 3 * w, 1, 0x0F00, [("src", 7), ("dstmate", 6)])
-        add("S", 3 * w, 4 * w, 1, 0xF000, [("src", 2), ("dstmate", 2)])
-        for q, h in enumerate((6, 7, 2, 3)):
-            add("A", q * w, (q + 1) * w, 2, 0xF << (4 * q), [("src", h)])
-        loads = [("B", 0, 1024), ("S", 0, 1024), ("A", 0, 1024)]
-        stores = [("S", 0, 512), ("B", 0, 1024), ("A", 0, 1024), ("S", 512, 1024)]
+    for k in (0, 1):
+        add("B", 2 * k, k, 0x000F, [("src", 4 + k), ("dstmate", 6 + k)])
+        add("B", 2 * k + 1, k, 0x00F0, [("src", 0), ("dstmate", 2 + k)])
+        add("A", 2 * k, k, 0x0F00, [("src", 6 + k)])
+        add("A", 2 * k + 1, k, 0xF000, [("src", 2 + k)])
+        add("S", 2 * k, 2, 0x000F << (8 * k), [("src", 4)])
+        add("S", 2 * k + 1, 2, 0x00F0 << (8 * k), [("src", 2)])
+    loads = [("B", 0, 512), ("A", 0, 512), ("B", 512, 1024), ("A", 512, 1024), ("S", 0, 1024)]
+    stores = [("A", 0, 1024), ("B", 0, 512), ("S", 0, 512), ("B", 512, 1024), ("S", 512, 1024)]
     return pieces, loads, stores
 
 
@@ -84,7 +69,7 @@ def build(cores):
                     mask = 0xFFFF if a // 8 == b // 8 else 0x00FF
                 sem = nsem.get(b, 0)
                 nsem[b] = sem + 1
-                hop = dict(frm=a, to=b, src=src, dst=dst, mask=mask, sem=sem, prev=prev, first=(h == 0),
+                hop = dict(frm=a, to=b, src=src, dst=dst, mask=mask, sem=sem, prev=prev,
                            last=(h == len(seq) - 2), wave=p["wave"], role=p["role"], c0=p["c0"], c1=p["c1"], s=s, d=d)
                 hops.append(hop)
                 prev = hop
@@ -99,8 +84,7 @@ def rank_program(g, core, T, topo):
     if not mine:
         return
     arr = [T.sem.a0, T.sem.a1, T.sem.a2, T.sem.a3, T.sem.a4, T.sem.a5, T.sem.a6, T.sem.a7,
-           T.sem.a8, T.sem.a9, T.sem.a10, T.sem.a11, T.sem.a12, T.sem.a13, T.sem.a14, T.sem.a15,
-           T.sem.a16, T.sem.a17, T.sem.a18, T.sem.a19, T.sem.a20, T.sem.a21, T.sem.a22, T.sem.a23]
+           T.sem.a8, T.sem.a9, T.sem.a10, T.sem.a11]
     buf = {"out": T.out, "land": T.land, "rel": T.rel}
 
     def ap(spec):
@@ -129,26 +113,15 @@ def rank_program(g, core, T, topo):
         g.wait_ge(T.sem.sent, sent)
         return
 
-    lds = [T.sem.ld0, T.sem.ld1, T.sem.ld2, T.sem.ld3, T.sem.ld4, T.sem.ld5, T.sem.ld6, T.sem.ld7]
-    waves = sorted(set(h["wave"] for h in mine))
-    nld, ldw = {}, {}
+    lds = [T.sem.ld0, T.sem.ld1, T.sem.ld2]
+    nld = {}
     for role, a, b in loads:
+        o = peer(role, r) * NB
         wave = min(h["wave"] for h in mine if h["role"] == role and a <= h["c0"] and h["c1"] <= b)
         nld[wave] = nld.get(wave, 0) + 1
-        ldw.setdefault(wave, []).append((role, a, b))
-
-    def load(wave):
-        for role, a, b in ldw.get(wave, []):
-            o = peer(role, r) * NB
-            g.dma_start(T.out[:, o + a:o + b], T.x[:, o + a:o + b]).then_inc(lds[wave], 16)
-
-    for wave in waves[:AHEAD]:
-        load(wave)
-    for i, wave in enumerate(waves):
-        if i + AHEAD < len(waves):
-            load(waves[i + AHEAD])
-        if wave in nld:
-            g.wait_ge(lds[wave], 16 * nld[wave])
+        g.dma_start(T.out[:, o + a:o + b], T.x[:, o + a:o + b]).then_inc(lds[wave], 16)
+    for wave in sorted(nld):
+        g.wait_ge(lds[wave], 16 * nld[wave])
         sent += send([h for h in mine if h["wave"] == wave])
     g.dma_start(T.y[:, r * NB:(r + 1) * NB], T.x[:, r * NB:(r + 1) * NB]).then_inc(T.sem.st, 16)
     for role, a, b in stores:

import concourse.bass as bass

NB = 1024

SCRATCH = {
    "out": ("sbuf", [128, 4096], "float32"),
    "land": ("sbuf", [128, 4096], "float32"),
    "rel": ("sbuf", [128, 1024], "float32"),
}
SEMAPHORES = ["ld0", "ld1", "ld2", "st", "sent",
              "a0", "a1", "a2", "a3", "a4", "a5", "a6", "a7", "a8", "a9", "a10", "a11"]


def peer(role, s):
    if role == "S":
        return s ^ 2
    if role == "A":
        return s ^ 1
    return 3 - s


def design():
    pieces = []

    def add(role, q, wave, mask0, relays):
        pieces.append(dict(role=role, c0=q * w, c1=(q + 1) * w, wave=wave, mask0=mask0, relays=relays))

    w = NB // 4
    for k in (0, 1):
        add("B", 2 * k, k, 0x000F, [("src", 4 + k), ("dstmate", 6 + k)])
        add("B", 2 * k + 1, k, 0x00F0, [("src", 0), ("dstmate", 2 + k)])
        add("A", 2 * k, k, 0x0F00, [("src", 6 + k)])
        add("A", 2 * k + 1, k, 0xF000, [("src", 2 + k)])
        add("S", 2 * k, 2, 0x000F << (8 * k), [("src", 4)])
        add("S", 2 * k + 1, 2, 0x00F0 << (8 * k), [("src", 2)])
    loads = [("B", 0, 512), ("A", 0, 512), ("B", 512, 1024), ("A", 512, 1024), ("S", 0, 1024)]
    stores = [("A", 0, 1024), ("B", 0, 512), ("S", 0, 512), ("B", 512, 1024), ("S", 512, 1024)]
    return pieces, loads, stores


def bits(m):
    return bin(m).count("1")


def build(cores):
    pieces, loads, stores = design()
    slot, nsem, hops = {}, {}, []
    for s in range(4):
        for p in pieces:
            d = peer(p["role"], s)
            seq = [cores[s]]
            for where, k in p["relays"]:
                ch = cores[s] // 8 if where == "src" else (cores[d] // 8) ^ 1
                seq.append(ch * 8 + k)
            seq.append(cores[d])
            src = ("out", d * NB + p["c0"], d * NB + p["c1"])
            prev = None
            for h in range(len(seq) - 1):
                a, b = seq[h], seq[h + 1]
                if h == len(seq) - 2:
                    dst = ("land", s * NB + p["c0"], s * NB + p["c1"])
                else:
                    o = slot.get(b, 0)
                    slot[b] = o + p["c1"] - p["c0"]
                    dst = ("rel", o, slot[b])
                if h == 0:
                    mask = p["mask0"]
                else:
                    mask = 0xFFFF if a // 8 == b // 8 else 0x00FF
                sem = nsem.get(b, 0)
                nsem[b] = sem + 1
                hop = dict(frm=a, to=b, src=src, dst=dst, mask=mask, sem=sem, prev=prev,
                           last=(h == len(seq) - 2), wave=p["wave"], role=p["role"], c0=p["c0"], c1=p["c1"], s=s, d=d)
                hops.append(hop)
                prev = hop
                src = dst
    return hops, loads, stores


def rank_program(g, core, T, topo):
    cores = list(T.cores)
    hops, loads, stores = build(cores)
    mine = [h for h in hops if h["frm"] == core]
    if not mine:
        return
    arr = [T.sem.a0, T.sem.a1, T.sem.a2, T.sem.a3, T.sem.a4, T.sem.a5, T.sem.a6, T.sem.a7,
           T.sem.a8, T.sem.a9, T.sem.a10, T.sem.a11]
    buf = {"out": T.out, "land": T.land, "rel": T.rel}

    def ap(spec):
        return buf[spec[0]][:, spec[1]:spec[2]]

    def send(group):
        if len(group) == 1:
            h = group[0]
            rid, pid, se = topo.addr(h["to"])
            g.remote_dma(ap(h["dst"]), ap(h["src"]), arr[h["sem"]], T.sem.sent, pid, rid, h["mask"])
        else:
            trs = []
            for h in group:
                rid, pid, se = topo.addr(h["to"])
                trs.append(bass.RemoteDMATransfer(dst_ids=[bass.DstId(rid=rid, pnc=pid)], dma_engine_mask=h["mask"],
                                                  remote_sem=arr[h["sem"]], src=ap(h["src"]), dst=ap(h["dst"])))
            g.remote_dma_fused(trs, local_sem=T.sem.sent)
        return sum(bits(h["mask"]) for h in group)

    sent = 0
    r = T.rank_of(core)
    if r is None:
        for h in sorted(mine, key=lambda h: h["wave"]):
            g.wait_ge(arr[h["prev"]["sem"]], bits(h["prev"]["mask"]))
            sent += send([h])
        g.wait_ge(T.sem.sent, sent)
        return

    lds = [T.sem.ld0, T.sem.ld1, T.sem.ld2]
    nld = {}
    for role, a, b in loads:
        o = peer(role, r) * NB
        wave = min(h["wave"] for h in mine if h["role"] == role and a <= h["c0"] and h["c1"] <= b)
        nld[wave] = nld.get(wave, 0) + 1
        g.dma_start(T.out[:, o + a:o + b], T.x[:, o + a:o + b]).then_inc(lds[wave], 16)
    for wave in sorted(nld):
        g.wait_ge(lds[wave], 16 * nld[wave])
        sent += send([h for h in mine if h["wave"] == wave])
    g.dma_start(T.y[:, r * NB:(r + 1) * NB], T.x[:, r * NB:(r + 1) * NB]).then_inc(T.sem.st, 16)
    for role, a, b in stores:
        s = peer(role, r)
        for h in hops:
            if h["last"] and h["to"] == core and h["s"] == s and a <= h["c0"] and h["c1"] <= b:
                g.wait_ge(arr[h["sem"]], bits(h["mask"]))
        g.dma_start(T.y[:, s * NB + a:s * NB + b], T.land[:, s * NB + a:s * NB + b]).then_inc(T.sem.st, 16)
    g.wait_ge(T.sem.st, 16 * (len(stores) + 1))
    g.wait_ge(T.sem.sent, sent)
